import numpy as np
import ml_dtypes


def mxq(x, axis, fmt="e4m3"):
    dtype, down = {"e4m3": (ml_dtypes.float8_e4m3fn, 7), "e5m2": (ml_dtypes.float8_e5m2, 14)}[fmt]
    v = np.moveaxis(np.asarray(x, np.float32).astype(ml_dtypes.bfloat16).astype(np.float64), axis, -1)
    blocks = v.reshape(v.shape[:-1] + (-1, 32))
    amax = np.abs(blocks).max(-1, keepdims=True)
    byte = np.maximum(np.where(amax > 0, np.frexp(amax)[1] - 1 + 127, 0) - down, 1)
    scale = np.exp2(byte - 127.0)
    codes = (blocks / scale).astype(np.float32).astype(dtype).astype(np.float64)
    return np.moveaxis((codes * scale).reshape(v.shape), -1, axis)


WIDE = False


def mx_kscale(k):
    if not WIDE:
        return np.ones(k)
    levels = np.array([10, -10, 5, -5, 0])
    if k % 512:
        return np.exp2(np.random.permutation(np.resize(levels, k // 32))).repeat(32)
    a = np.empty((k // 512, 16))
    for p in range(k // 512):
        a[p, :8] = np.random.permutation(np.resize(levels, 8))
        for g in range(8):
            far = levels[np.abs(levels - a[p, g]) >= 10]
            a[p, g + 8] = far[np.random.randint(len(far))]
    return np.exp2(a.ravel()).repeat(32)


def f64(x):
    return np.asarray(x).astype(np.float64)


def striped(idx):
    return np.tile(idx.reshape(-1, 16).T, (8, 1)).astype(np.uint16)


def unstriped(offs):
    return offs[:16].T.reshape(-1).astype(np.int64)


E2M1 = np.array([0.0, 0.5, 1.0, 1.5, 2.0, 3.0, 4.0, 6.0, -0.0, -0.5, -1.0, -1.5, -2.0, -3.0, -4.0, -6.0])


def pack_weight(w, fmt):
    k, n = w.shape
    w = f64(np.asarray(w, np.float32).astype(ml_dtypes.bfloat16)).reshape(k // 32, 32, n)
    amax = np.abs(w).max(1)
    if fmt == "e4m3":
        byte = np.frexp(amax)[1] - 1 + 127 - 7
    else:
        mant, ex = np.frexp(amax / 6.0)
        byte = np.where(mant > 0.5, ex, ex - 1) + 127
    byte = np.clip(np.where(amax > 0, byte, 1), 1, 254)
    scaled = (w * np.exp2(127.0 - byte)[:, None, :]).reshape(k, n).astype(np.float32)
    by_word = np.ascontiguousarray(scaled.reshape(k // 512, 128, 4, n).transpose(0, 1, 3, 2))
    if fmt == "e4m3":
        words = by_word.astype(ml_dtypes.float8_e4m3fn).view(np.uint8)
    else:
        c = by_word.astype(ml_dtypes.float4_e2m1fn).view(np.uint8) & 0xF
        words = (c[..., 0::2] | (c[..., 1::2] << 4)).reshape(k // 512, 128, 2 * n)
    return np.ascontiguousarray(words), np.ascontiguousarray(byte.astype(np.uint8).reshape(k // 512, 16, n))


def unpack_weight(words, scales, fmt):
    g, _, n = scales.shape
    words = np.ascontiguousarray(words).reshape(g, 128, n, -1)
    if fmt == "e4m3":
        vals = words.view(ml_dtypes.float8_e4m3fn).astype(np.float64)
    else:
        nib = np.empty((g, 128, n, 4), np.uint8)
        nib[..., 0::2] = words & 0xF
        nib[..., 1::2] = words >> 4
        vals = E2M1[nib]
    vals = vals * np.repeat(np.exp2(scales.astype(np.float64) - 127.0), 8, axis=1)[..., None]
    return vals.transpose(0, 1, 3, 2).reshape(g * 512, n)


def split(x):
    m, e = np.frexp(f64(x))
    hi = np.ldexp(np.trunc(16.0 * m) / 16.0, e)
    return hi, f64(x) - hi


K, M, T, S = 512, 256, 2048, 1024


def setup_inputs():
    n = np.random.standard_normal
    s = mx_kscale(K)[:, None]
    v = pack_weight(n((K, T)) * s, "e4m3")
    return {
        "tab_words": v[0],
        "tab_scales": v[1],
        "w": (n((K, M)) / np.sqrt(K) / s).astype(np.float32),
        "rT": n((M, T)).astype(np.float32),
        "offs": striped(np.random.permutation(T)[:S]),
    }


def reference(tab_words, tab_scales, w, rT, offs):
    tab_ = unpack_weight(tab_words, tab_scales, "e4m3")[:, unstriped(offs)]
    w_hi, w_lo = split(w)
    w_hi_, w_lo_ = mxq(w_hi, 0, "e4m3"), mxq(w_lo, 0, "e4m3")
    y = w_hi_.T @ tab_ + w_lo_.T @ tab_
    return (y) + f64(rT)[:, unstriped(offs)]

@@ -1,0 +1,110 @@
+from contextlib import ExitStack
+
+import concourse.mybir as mybir
+
+K, M, T, S = 512, 256, 2048, 1024
+FLOPS = 2 * 2 * K * M * S
+
+F32 = mybir.dt.float32
+BF16 = mybir.dt.bfloat16
+I32 = mybir.dt.int32
+U32 = mybir.dt.uint32
+U16 = mybir.dt.uint16
+U8 = mybir.dt.uint8
+FP8X4 = mybir.dt.float8_e4m3fn_x4
+ALU = mybir.AluOpType
+
+P = 128
+PACK = 4
+N_TILE = 512
+HI_MASK = -(1 << 20)
+
+
+def tile_list_tabres_none_kernel(tc, tab_words, tab_scales, w, rT, offs, out):
+    nc = tc.nc
+    with ExitStack() as ctx:
+        keep = ctx.enter_context(tc.tile_pool(name="keep", bufs=1))
+        psum = ctx.enter_context(tc.psum_pool(name="psum", bufs=1))
+
+        offsets = keep.tile([P, S // 16], U16, name="offsets")
+        w_raw = keep.tile([P, PACK, M], F32, name="w_raw")
+        scale_win = keep.tile([P, T // 4], I32, name="scale_win")
+        word_win = keep.tile([P, T], I32, name="word_win")
+        res_win = [keep.tile([P, T], F32, name=f"res_win{m}") for m in range(2)]
+
+        nc.gpsimd.memset(scale_win[:], 0)
+        nc.sync.dma_start(out=w_raw[:], in_=w.rearrange("(p j) n -> p j n", j=PACK))
+        nc.sync.dma_start(offsets[:], offs)
+        scale_rows = tab_scales[0].bitcast(I32)
+        for r in range(4):
+            nc.sync.dma_start(out=scale_win[r:P:32, :], in_=scale_rows[r:16:4, :])
+        nc.sync.dma_start(out=word_win[:], in_=tab_words[0].rearrange("p t i -> p (t i)").bitcast(I32))
+        for m in range(2):
+            nc.sync.dma_start(out=res_win[m][:], in_=rT[m * P : (m + 1) * P, :])
+
+        def lookup(window, j0, j1):
+            return window.indirect(offsets[:, j0 // 16 : j1 // 16])
+
+        hi_bits = keep.tile([P, M, PACK], I32, name="hi_bits", tag="reuse", align_bytes=64)
+        nc.vector.tensor_scalar(
+            out=hi_bits[:], in0=w_raw[:].bitcast(I32).rearrange("p j n -> p n j"),
+            scalar1=HI_MASK, scalar2=None, op0=ALU.bitwise_and,
+        )
+        w_bf = keep.tile([P, 2, M, PACK], BF16, name="w_bf", align_bytes=64)
+        nc.scalar.copy(out=w_bf[:, 0], in_=hi_bits[:].bitcast(F32))
+        nc.gpsimd.tensor_tensor(
+            out=w_bf[:, 1], in0=w_raw[:].rearrange("p j n -> p n j"), in1=hi_bits[:].bitcast(F32), op=ALU.subtract
+        )
+
+        v_scales = keep.tile([P, S], U8, name="v_scales", align_bytes=64)
+        nc.vector.tensor_copy(out=v_scales[:], in_=lookup(scale_win[:].bitcast(U8), 0, S))
+
+        w_codes = keep.tile([P, 2 * M], U32, name="w_codes", align_bytes=64)
+        w_scales = keep.tile([P, 2 * M], U8, name="w_scales", align_bytes=64)
+        nc.vector.quantize_mx(
+            out=w_codes[:].bitcast(FP8X4), scales=w_scales[:], in_=w_bf[:].rearrange("p h n j -> p (h n j)")
+        )
+
+        v_words = [
+            keep.tile([P, N_TILE], U32, name="v_words0", align_bytes=64),
+            keep.tile([P, N_TILE], U32, name="v_words1", tag="reuse", align_bytes=64),
+        ]
+        acc = {}
+        for h in range(2):
+            nc.vector.tensor_copy(out=v_words[h][:], in_=lookup(word_win[:].bitcast(U32), h * N_TILE, (h + 1) * N_TILE))
+            for m in range(2):
+                acc[m, h] = psum.tile([P, N_TILE], F32, name=f"acc{m}{h}")
+                for part in range(2):
+                    c0 = part * M + m * P
+                    nc.tensor.matmul_mx(
+                        out=acc[m, h][:],
+                        lhsT=w_codes[:, c0 : c0 + P].bitcast(FP8X4),
+                        lhsT_scale=w_scales[:, c0 : c0 + P],
+                        rhs=v_words[h][:].bitcast(FP8X4),
+                        rhs_scale=v_scales[:, h * N_TILE : (h + 1) * N_TILE],
+                        start=(part == 0),
+                        stop=(part == 1),
+                    )
+
+        y_sb = {}
+        for m, h in ((0, 0), (0, 1), (1, 0)):
+            y_sb[m, h] = keep.tile([P, N_TILE], F32, name=f"y_sb{m}{h}")
+            nc.scalar.copy(out=y_sb[m, h][:], in_=acc[m, h][:])
+
+        for m, h in ((0, 0), (0, 1), (1, 0)):
+            picked = keep.tile([P, N_TILE], F32, name=f"picked{m}{h}")
+            nc.vector.tensor_copy(out=picked[:], in_=lookup(res_win[m][:], h * N_TILE, (h + 1) * N_TILE))
+            total = keep.tile([P, N_TILE], F32, name=f"total{m}{h}")
+            nc.gpsimd.tensor_tensor(out=total[:], in0=y_sb[m, h][:], in1=picked[:], op=ALU.add)
+            nc.sync.dma_start(out=out[m * P : (m + 1) * P, h * N_TILE : (h + 1) * N_TILE], in_=total[:])
+
+        half = N_TILE // 2
+        tail = [keep.tile([P, half], F32, name=f"tail{i}") for i in range(2)]
+        for i in range(2):
+            j0 = N_TILE + i * half
+            nc.vector.tensor_copy(out=tail[i][:], in_=lookup(res_win[1][:], j0, j0 + half))
+        for i in range(2):
+            j0 = N_TILE + i * half
+            total = keep.tile([P, half], F32, name=f"tail_total{i}")
+            nc.vector.tensor_tensor(out=total[:], in0=acc[1, 1][:, i * half : (i + 1) * half], in1=tail[i][:], op=ALU.add)
+            nc.sync.dma_start(out=out[P : 2 * P, j0 : j0 + half], in_=total[:])

@@ -16,7 +16,7 @@ ALU = mybir.AluOpType
 
 P = 128
 PACK = 4
-N_TILE = 512
+Q = 256
 HI_MASK = -(1 << 20)
 
 
@@ -32,12 +32,12 @@ def tile_list_tabres_none_kernel(tc, tab_words, tab_scales, w, rT, offs, out):
         word_win = keep.tile([P, T], I32, name="word_win")
         res_win = [keep.tile([P, T], F32, name=f"res_win{m}") for m in range(2)]
 
-        nc.gpsimd.memset(scale_win[:], 0)
-        nc.sync.dma_start(out=w_raw[:], in_=w.rearrange("(p j) n -> p j n", j=PACK))
+        nc.vector.memset(scale_win[:], 0)
         nc.sync.dma_start(offsets[:], offs)
         scale_rows = tab_scales[0].bitcast(I32)
         for r in range(4):
             nc.sync.dma_start(out=scale_win[r:P:32, :], in_=scale_rows[r:16:4, :])
+        nc.sync.dma_start(out=w_raw[:], in_=w.rearrange("(p j) n -> p j n", j=PACK))
         nc.sync.dma_start(out=word_win[:], in_=tab_words[0].rearrange("p t i -> p (t i)").bitcast(I32))
         for m in range(2):
             nc.sync.dma_start(out=res_win[m][:], in_=rT[m * P : (m + 1) * P, :])
@@ -45,66 +45,63 @@ def tile_list_tabres_none_kernel(tc, tab_words, tab_scales, w, rT, offs, out):
         def lookup(window, j0, j1):
             return window.indirect(offsets[:, j0 // 16 : j1 // 16])
 
-        hi_bits = keep.tile([P, M, PACK], I32, name="hi_bits", tag="reuse", align_bytes=64)
-        nc.vector.tensor_scalar(
-            out=hi_bits[:], in0=w_raw[:].bitcast(I32).rearrange("p j n -> p n j"),
-            scalar1=HI_MASK, scalar2=None, op0=ALU.bitwise_and,
-        )
-        w_bf = keep.tile([P, 2, M, PACK], BF16, name="w_bf", align_bytes=64)
-        nc.scalar.copy(out=w_bf[:, 0], in_=hi_bits[:].bitcast(F32))
-        nc.gpsimd.tensor_tensor(
-            out=w_bf[:, 1], in0=w_raw[:].rearrange("p j n -> p n j"), in1=hi_bits[:].bitcast(F32), op=ALU.subtract
-        )
-
         v_scales = keep.tile([P, S], U8, name="v_scales", align_bytes=64)
         nc.vector.tensor_copy(out=v_scales[:], in_=lookup(scale_win[:].bitcast(U8), 0, S))
 
-        w_codes = keep.tile([P, 2 * M], U32, name="w_codes", align_bytes=64)
-        w_scales = keep.tile([P, 2 * M], U8, name="w_scales", align_bytes=64)
-        nc.vector.quantize_mx(
-            out=w_codes[:].bitcast(FP8X4), scales=w_scales[:], in_=w_bf[:].rearrange("p h n j -> p (h n j)")
-        )
+        w_bf = []
+        for m in range(2):
+            w_cols = w_raw[:, :, m * P : (m + 1) * P].rearrange("p j n -> p n j")
+            hi_bits = keep.tile([P, P, PACK], I32, name=f"hi_bits{m}", tag=f"hi{m}", align_bytes=64)
+            nc.vector.tensor_scalar(
+                out=hi_bits[:], in0=w_raw[:].bitcast(I32)[:, :, m * P : (m + 1) * P].rearrange("p j n -> p n j"),
+                scalar1=HI_MASK, scalar2=None, op0=ALU.bitwise_and,
+            )
+            parts = keep.tile([P, 2, P, PACK], BF16, name=f"w_bf{m}", align_bytes=64)
+            nc.scalar.copy(out=parts[:, 0], in_=hi_bits[:].bitcast(F32))
+            nc.gpsimd.tensor_tensor(out=parts[:, 1], in0=w_cols, in1=hi_bits[:].bitcast(F32), op=ALU.subtract)
+            w_bf.append(parts)
 
-        v_words = [
-            keep.tile([P, N_TILE], U32, name="v_words0", align_bytes=64),
-            keep.tile([P, N_TILE], U32, name="v_words1", tag="reuse", align_bytes=64),
-        ]
-        acc = {}
-        for h in range(2):
-            nc.vector.tensor_copy(out=v_words[h][:], in_=lookup(word_win[:].bitcast(U32), h * N_TILE, (h + 1) * N_TILE))
-            for m in range(2):
-                acc[m, h] = psum.tile([P, N_TILE], F32, name=f"acc{m}{h}")
-                for part in range(2):
-                    c0 = part * M + m * P
-                    nc.tensor.matmul_mx(
-                        out=acc[m, h][:],
-                        lhsT=w_codes[:, c0 : c0 + P].bitcast(FP8X4),
-                        lhsT_scale=w_scales[:, c0 : c0 + P],
-                        rhs=v_words[h][:].bitcast(FP8X4),
-                        rhs_scale=v_scales[:, h * N_TILE : (h + 1) * N_TILE],
-                        start=(part == 0),
-                        stop=(part == 1),
-                    )
+        v_early = keep.tile([P, 2 * Q], U32, name="v_early", align_bytes=64)
+        v_late = keep.tile([P, 2 * Q], U32, name="v_late", tag="hi0", align_bytes=64)
+        v_words = [half[:, i * Q : (i + 1) * Q] for half in (v_early, v_late) for i in range(2)]
 
-        y_sb = {}
-        for m, h in ((0, 0), (0, 1), (1, 0)):
-            y_sb[m, h] = keep.tile([P, N_TILE], F32, name=f"y_sb{m}{h}")
-            nc.scalar.copy(out=y_sb[m, h][:], in_=acc[m, h][:])
+        def gather_words(q):
+            nc.vector.tensor_copy(out=v_words[q], in_=lookup(word_win[:].bitcast(U32), q * Q, (q + 1) * Q))
 
-        for m, h in ((0, 0), (0, 1), (1, 0)):
-            picked = keep.tile([P, N_TILE], F32, name=f"picked{m}{h}")
-            nc.vector.tensor_copy(out=picked[:], in_=lookup(res_win[m][:], h * N_TILE, (h + 1) * N_TILE))
-            total = keep.tile([P, N_TILE], F32, name=f"total{m}{h}")
-            nc.gpsimd.tensor_tensor(out=total[:], in0=y_sb[m, h][:], in1=picked[:], op=ALU.add)
-            nc.sync.dma_start(out=out[m * P : (m + 1) * P, h * N_TILE : (h + 1) * N_TILE], in_=total[:])
+        def quantize(m):
+            codes = keep.tile([P, 2 * P], U32, name=f"w_codes{m}", align_bytes=64)
+            scales = keep.tile([P, 2 * P], U8, name=f"w_scales{m}", align_bytes=64)
+            nc.vector.quantize_mx(
+                out=codes[:].bitcast(FP8X4), scales=scales[:], in_=w_bf[m][:].rearrange("p h n j -> p (h n j)")
+            )
+            return codes, scales
 
-        half = N_TILE // 2
-        tail = [keep.tile([P, half], F32, name=f"tail{i}") for i in range(2)]
-        for i in range(2):
-            j0 = N_TILE + i * half
-            nc.vector.tensor_copy(out=tail[i][:], in_=lookup(res_win[1][:], j0, j0 + half))
-        for i in range(2):
-            j0 = N_TILE + i * half
-            total = keep.tile([P, half], F32, name=f"tail_total{i}")
-            nc.vector.tensor_tensor(out=total[:], in0=acc[1, 1][:, i * half : (i + 1) * half], in1=tail[i][:], op=ALU.add)
-            nc.sync.dma_start(out=out[P : 2 * P, j0 : j0 + half], in_=total[:])
+        def block(m, q, codes, scales):
+            acc = psum.tile([P, Q], F32, name=f"acc{m}{q}")
+            for part in range(2):
+                nc.tensor.matmul_mx(
+                    out=acc[:],
+                    lhsT=codes[:, part * P : (part + 1) * P].bitcast(FP8X4),
+                    lhsT_scale=scales[:, part * P : (part + 1) * P],
+                    rhs=v_words[q].bitcast(FP8X4),
+                    rhs_scale=v_scales[:, q * Q : (q + 1) * Q],
+                    start=(part == 0),
+                    stop=(part == 1),
+                )
+            y_sb = keep.tile([P, Q], F32, name=f"y_sb{m}{q}")
+            nc.scalar.copy(out=y_sb[:], in_=acc[:])
+            total = keep.tile([P, Q], F32, name=f"total{m}{q}")
+            nc.vector.tensor_tensor(
+                out=total[:], in0=lookup(res_win[m][:], q * Q, (q + 1) * Q), in1=y_sb[:], op=ALU.add
+            )
+            nc.sync.dma_start(out=out[m * P : (m + 1) * P, q * Q : (q + 1) * Q], in_=total[:])
+
+        gather_words(0)
+        gather_words(1)
+        first = quantize(0)
+        gather_words(2)
+        gather_words(3)
+        second = quantize(1)
+        for m, (codes, scales) in enumerate((first, second)):
+            for q in range(S // Q):
+                block(m, q, codes, scales)

@@ -16,7 +16,8 @@ ALU = mybir.AluOpType
 
 P = 128
 PACK = 4
-Q = 256
+PRODUCT_CUTS = ((0, 256, 512, 768, 1024), (0, 256, 512, 1024))
+SUM_CUTS = ((0, 256, 512, 768, 1024), (0, 512, 896, 1024))
 HI_MASK = -(1 << 20)
 
 
@@ -61,12 +62,10 @@ def tile_list_tabres_none_kernel(tc, tab_words, tab_scales, w, rT, offs, out):
             nc.gpsimd.tensor_tensor(out=parts[:, 1], in0=w_cols, in1=hi_bits[:].bitcast(F32), op=ALU.subtract)
             w_bf.append(parts)
 
-        v_early = keep.tile([P, 2 * Q], U32, name="v_early", align_bytes=64)
-        v_late = keep.tile([P, 2 * Q], U32, name="v_late", tag="hi0", align_bytes=64)
-        v_words = [half[:, i * Q : (i + 1) * Q] for half in (v_early, v_late) for i in range(2)]
+        v_words = keep.tile([P, S], U32, name="v_words", tag="hi0", align_bytes=64)
 
-        def gather_words(q):
-            nc.vector.tensor_copy(out=v_words[q], in_=lookup(word_win[:].bitcast(U32), q * Q, (q + 1) * Q))
+        def gather_words(j0, j1):
+            nc.vector.tensor_copy(out=v_words[:, j0:j1], in_=lookup(word_win[:].bitcast(U32), j0, j1))
 
         def quantize(m):
             codes = keep.tile([P, 2 * P], U32, name=f"w_codes{m}", align_bytes=64)
@@ -76,32 +75,34 @@ def tile_list_tabres_none_kernel(tc, tab_words, tab_scales, w, rT, offs, out):
             )
             return codes, scales
 
-        def block(m, q, codes, scales):
-            acc = psum.tile([P, Q], F32, name=f"acc{m}{q}")
+        def project(m, j0, j1, codes, scales, y_sb):
+            acc = psum.tile([P, j1 - j0], F32, name=f"acc{m}_{j0}")
             for part in range(2):
                 nc.tensor.matmul_mx(
                     out=acc[:],
                     lhsT=codes[:, part * P : (part + 1) * P].bitcast(FP8X4),
                     lhsT_scale=scales[:, part * P : (part + 1) * P],
-                    rhs=v_words[q].bitcast(FP8X4),
-                    rhs_scale=v_scales[:, q * Q : (q + 1) * Q],
+                    rhs=v_words[:, j0:j1].bitcast(FP8X4),
+                    rhs_scale=v_scales[:, j0:j1],
                     start=(part == 0),
                     stop=(part == 1),
                 )
-            y_sb = keep.tile([P, Q], F32, name=f"y_sb{m}{q}")
-            nc.scalar.copy(out=y_sb[:], in_=acc[:])
-            total = keep.tile([P, Q], F32, name=f"total{m}{q}")
-            nc.vector.tensor_tensor(
-                out=total[:], in0=lookup(res_win[m][:], q * Q, (q + 1) * Q), in1=y_sb[:], op=ALU.add
-            )
-            nc.sync.dma_start(out=out[m * P : (m + 1) * P, q * Q : (q + 1) * Q], in_=total[:])
+            nc.scalar.copy(out=y_sb[:, j0:j1], in_=acc[:])
 
-        gather_words(0)
-        gather_words(1)
+        def finish(m, j0, j1, y_sb):
+            total = keep.tile([P, j1 - j0], F32, name=f"total{m}_{j0}")
+            nc.vector.tensor_tensor(out=total[:], in0=lookup(res_win[m][:], j0, j1), in1=y_sb[:, j0:j1], op=ALU.add)
+            nc.sync.dma_start(out=out[m * P : (m + 1) * P, j0:j1], in_=total[:])
+
         first = quantize(0)
-        gather_words(2)
-        gather_words(3)
+        for j0 in range(0, S, 256):
+            gather_words(j0, j0 + 256)
         second = quantize(1)
         for m, (codes, scales) in enumerate((first, second)):
-            for q in range(S // Q):
-                block(m, q, codes, scales)
+            y_sb = keep.tile([P, S], F32, name=f"y_sb{m}")
+            cuts = PRODUCT_CUTS[m]
+            for j0, j1 in zip(cuts, cuts[1:]):
+                project(m, j0, j1, codes, scales, y_sb)
+            cuts = SUM_CUTS[m]
+            for j0, j1 in zip(cuts, cuts[1:]):
+                finish(m, j0, j1, y_sb)

@@ -16,8 +16,10 @@ ALU = mybir.AluOpType
 
 P = 128
 PACK = 4
+Q = 256
 PRODUCT_CUTS = ((0, 256, 512, 768, 1024), (0, 256, 512, 1024))
-SUM_CUTS = ((0, 256, 512, 768, 1024), (0, 512, 896, 1024))
+SUM_CUTS = ((0, 256, 512, 1024), (0, 512, 896, 1024))
+PAIR_MASK = 0xFFF0FFF0 - (1 << 32)
 HI_MASK = -(1 << 20)
 
 
@@ -28,17 +30,19 @@ def tile_list_tabres_none_kernel(tc, tab_words, tab_scales, w, rT, offs, out):
         psum = ctx.enter_context(tc.psum_pool(name="psum", bufs=1))
 
         offsets = keep.tile([P, S // 16], U16, name="offsets")
-        w_raw = keep.tile([P, PACK, M], F32, name="w_raw")
+        w_raw = [keep.tile([P, PACK, P], F32, name=f"w_raw{m}", tag=f"w_raw{m}") for m in range(2)]
         scale_win = keep.tile([P, T // 4], I32, name="scale_win")
         word_win = keep.tile([P, T], I32, name="word_win")
         res_win = [keep.tile([P, T], F32, name=f"res_win{m}") for m in range(2)]
 
         nc.vector.memset(scale_win[:], 0)
+        w_rows = w.rearrange("(p j) n -> p j n", j=PACK)
+        nc.sync.dma_start(out=w_raw[0][:], in_=w_rows[:, :, 0:P])
         nc.sync.dma_start(offsets[:], offs)
         scale_rows = tab_scales[0].bitcast(I32)
         for r in range(4):
             nc.sync.dma_start(out=scale_win[r:P:32, :], in_=scale_rows[r:16:4, :])
-        nc.sync.dma_start(out=w_raw[:], in_=w.rearrange("(p j) n -> p j n", j=PACK))
+        nc.sync.dma_start(out=w_raw[1][:], in_=w_rows[:, :, P:M])
         nc.sync.dma_start(out=word_win[:], in_=tab_words[0].rearrange("p t i -> p (t i)").bitcast(I32))
         for m in range(2):
             nc.sync.dma_start(out=res_win[m][:], in_=rT[m * P : (m + 1) * P, :])
@@ -46,26 +50,31 @@ def tile_list_tabres_none_kernel(tc, tab_words, tab_scales, w, rT, offs, out):
         def lookup(window, j0, j1):
             return window.indirect(offsets[:, j0 // 16 : j1 // 16])
 
+        w_bf = [keep.tile([P, 2, P, PACK], BF16, name=f"w_bf{m}", align_bytes=64) for m in range(2)]
+
+        def woven(view):
+            return view.rearrange("p j n -> p n j")
+
+        hi_bits = keep.tile([P, P, PACK], I32, name="hi_bits", tag="early", align_bytes=64)
+        nc.vector.tensor_scalar(
+            out=hi_bits[:], in0=woven(w_raw[0][:].bitcast(I32)), scalar1=HI_MASK, scalar2=None, op0=ALU.bitwise_and
+        )
+        nc.scalar.copy(out=w_bf[0][:, 0], in_=hi_bits[:].bitcast(F32))
+        nc.gpsimd.tensor_tensor(out=w_bf[0][:, 1], in0=woven(w_raw[0][:]), in1=hi_bits[:].bitcast(F32), op=ALU.subtract)
+
         v_scales = keep.tile([P, S], U8, name="v_scales", align_bytes=64)
         nc.vector.tensor_copy(out=v_scales[:], in_=lookup(scale_win[:].bitcast(U8), 0, S))
 
-        w_bf = []
-        for m in range(2):
-            w_cols = w_raw[:, :, m * P : (m + 1) * P].rearrange("p j n -> p n j")
-            hi_bits = keep.tile([P, P, PACK], I32, name=f"hi_bits{m}", tag=f"hi{m}", align_bytes=64)
-            nc.vector.tensor_scalar(
-                out=hi_bits[:], in0=w_raw[:].bitcast(I32)[:, :, m * P : (m + 1) * P].rearrange("p j n -> p n j"),
-                scalar1=HI_MASK, scalar2=None, op0=ALU.bitwise_and,
-            )
-            parts = keep.tile([P, 2, P, PACK], BF16, name=f"w_bf{m}", align_bytes=64)
-            nc.scalar.copy(out=parts[:, 0], in_=hi_bits[:].bitcast(F32))
-            nc.gpsimd.tensor_tensor(out=parts[:, 1], in0=w_cols, in1=hi_bits[:].bitcast(F32), op=ALU.subtract)
-            w_bf.append(parts)
-
-        v_words = keep.tile([P, S], U32, name="v_words", tag="hi0", align_bytes=64)
-
-        def gather_words(j0, j1):
-            nc.vector.tensor_copy(out=v_words[:, j0:j1], in_=lookup(word_win[:].bitcast(U32), j0, j1))
+        upper = keep.tile([P, P, PACK], BF16, name="upper", align_bytes=64)
+        nc.scalar.copy(
+            out=upper[:], in_=w_raw[1][:].bitcast(BF16).rearrange("p j (n t) -> p n j t", t=2)[:, :, :, 1]
+        )
+        nc.vector.tensor_scalar(
+            out=w_bf[1][:, 0].rearrange("p n j -> p (n j)").bitcast(I32),
+            in0=upper[:].rearrange("p n j -> p (n j)").bitcast(I32),
+            scalar1=PAIR_MASK, scalar2=None, op0=ALU.bitwise_and,
+        )
+        nc.gpsimd.tensor_tensor(out=w_bf[1][:, 1], in0=woven(w_raw[1][:]), in1=w_bf[1][:, 0], op=ALU.subtract)
 
         def quantize(m):
             codes = keep.tile([P, 2 * P], U32, name=f"w_codes{m}", align_bytes=64)
@@ -74,6 +83,12 @@ def tile_list_tabres_none_kernel(tc, tab_words, tab_scales, w, rT, offs, out):
                 out=codes[:].bitcast(FP8X4), scales=scales[:], in_=w_bf[m][:].rearrange("p h n j -> p (h n j)")
             )
             return codes, scales
+
+        first = quantize(0)
+        v_words = keep.tile([P, S], U32, name="v_words", tag="early", align_bytes=64)
+        for j0 in range(0, S, Q):
+            nc.vector.tensor_copy(out=v_words[:, j0 : j0 + Q], in_=lookup(word_win[:].bitcast(U32), j0, j0 + Q))
+        second = quantize(1)
 
         def project(m, j0, j1, codes, scales, y_sb):
             acc = psum.tile([P, j1 - j0], F32, name=f"acc{m}_{j0}")
@@ -89,20 +104,16 @@ def tile_list_tabres_none_kernel(tc, tab_words, tab_scales, w, rT, offs, out):
                 )
             nc.scalar.copy(out=y_sb[:, j0:j1], in_=acc[:])
 
-        def finish(m, j0, j1, y_sb):
-            total = keep.tile([P, j1 - j0], F32, name=f"total{m}_{j0}")
-            nc.vector.tensor_tensor(out=total[:], in0=lookup(res_win[m][:], j0, j1), in1=y_sb[:, j0:j1], op=ALU.add)
-            nc.sync.dma_start(out=out[m * P : (m + 1) * P, j0:j1], in_=total[:])
+        def finish(m, j0, j1, y_sb, total):
+            nc.vector.tensor_tensor(out=total, in0=lookup(res_win[m][:], j0, j1), in1=y_sb[:, j0:j1], op=ALU.add)
+            nc.sync.dma_start(out=out[m * P : (m + 1) * P, j0:j1], in_=total)
 
-        first = quantize(0)
-        for j0 in range(0, S, 256):
-            gather_words(j0, j0 + 256)
-        second = quantize(1)
         for m, (codes, scales) in enumerate((first, second)):
             y_sb = keep.tile([P, S], F32, name=f"y_sb{m}")
+            total = keep.tile([P, S], F32, name=f"total{m}")
             cuts = PRODUCT_CUTS[m]
             for j0, j1 in zip(cuts, cuts[1:]):
                 project(m, j0, j1, codes, scales, y_sb)
             cuts = SUM_CUTS[m]
             for j0, j1 in zip(cuts, cuts[1:]):
-                finish(m, j0, j1, y_sb)
+                finish(m, j0, j1, y_sb, total[:, j0:j1])

@@ -13,14 +13,21 @@ U16 = mybir.dt.uint16
 U8 = mybir.dt.uint8
 FP8X4 = mybir.dt.float8_e4m3fn_x4
 ALU = mybir.AluOpType
+COPY = mybir.ActivationFunctionType.Copy
 
 P = 128
 PACK = 4
-Q = 256
+GROUP = 16
+QUADRANT = 32
+SCALE_ROWS = K // 32
+
+WORD_PIECE = 256
 PRODUCT_CUTS = ((0, 256, 512, 768, 1024), (0, 256, 512, 1024))
 SUM_CUTS = ((0, 256, 512, 1024), (0, 512, 896, 1024))
-PAIR_MASK = 0xFFF0FFF0 - (1 << 32)
-HI_MASK = -(1 << 20)
+
+DROPPED_BITS = 20
+HI_MASK = -(1 << DROPPED_BITS)
+ROUND_DOWN = -15.0 / 32.0
 
 
 def tile_list_tabres_none_kernel(tc, tab_words, tab_scales, w, rT, offs, out):
@@ -29,69 +36,71 @@ def tile_list_tabres_none_kernel(tc, tab_words, tab_scales, w, rT, offs, out):
         keep = ctx.enter_context(tc.tile_pool(name="keep", bufs=1))
         psum = ctx.enter_context(tc.psum_pool(name="psum", bufs=1))
 
-        offsets = keep.tile([P, S // 16], U16, name="offsets")
-        w_raw = [keep.tile([P, PACK, P], F32, name=f"w_raw{m}", tag=f"w_raw{m}") for m in range(2)]
+        offsets = keep.tile([P, S // GROUP], U16, name="offsets")
+        w_raw = [keep.tile([P, PACK, P], F32, name=f"w_raw{half}", tag=f"w_raw{half}") for half in range(2)]
         scale_win = keep.tile([P, T // 4], I32, name="scale_win")
         word_win = keep.tile([P, T], I32, name="word_win")
-        res_win = [keep.tile([P, T], F32, name=f"res_win{m}") for m in range(2)]
+        res_win = [keep.tile([P, T], F32, name=f"res_win{half}") for half in range(2)]
 
         nc.vector.memset(scale_win[:], 0)
-        w_rows = w.rearrange("(p j) n -> p j n", j=PACK)
+
+        w_rows = w.rearrange("(p t) n -> p t n", t=PACK)
         nc.sync.dma_start(out=w_raw[0][:], in_=w_rows[:, :, 0:P])
         nc.sync.dma_start(offsets[:], offs)
         scale_rows = tab_scales[0].bitcast(I32)
         for r in range(4):
-            nc.sync.dma_start(out=scale_win[r:P:32, :], in_=scale_rows[r:16:4, :])
+            nc.sync.dma_start(out=scale_win[r:P:QUADRANT, :], in_=scale_rows[r:SCALE_ROWS:4, :])
         nc.sync.dma_start(out=w_raw[1][:], in_=w_rows[:, :, P:M])
-        nc.sync.dma_start(out=word_win[:], in_=tab_words[0].rearrange("p t i -> p (t i)").bitcast(I32))
-        for m in range(2):
-            nc.sync.dma_start(out=res_win[m][:], in_=rT[m * P : (m + 1) * P, :])
+        nc.sync.dma_start(out=word_win[:], in_=tab_words[0].rearrange("p c t -> p (c t)").bitcast(I32))
+        for half in range(2):
+            nc.sync.dma_start(out=res_win[half][:], in_=rT[half * P : (half + 1) * P, :])
 
         def lookup(window, j0, j1):
-            return window.indirect(offsets[:, j0 // 16 : j1 // 16])
+            return window.indirect(offsets[:, j0 // GROUP : j1 // GROUP])
 
-        w_bf = [keep.tile([P, 2, P, PACK], BF16, name=f"w_bf{m}", align_bytes=64) for m in range(2)]
+        def k_last(view):
+            return view.rearrange("p t n -> p n t")
 
-        def woven(view):
-            return view.rearrange("p j n -> p n j")
+        w_bf = [keep.tile([P, 2, P, PACK], BF16, name=f"w_bf{half}", align_bytes=64) for half in range(2)]
 
-        hi_bits = keep.tile([P, P, PACK], I32, name="hi_bits", tag="early", align_bytes=64)
+        hi_bits = keep.tile([P, P, PACK], I32, name="hi_bits", tag="first_cut", align_bytes=64)
         nc.vector.tensor_scalar(
-            out=hi_bits[:], in0=woven(w_raw[0][:].bitcast(I32)), scalar1=HI_MASK, scalar2=None, op0=ALU.bitwise_and
+            out=hi_bits[:], in0=k_last(w_raw[0][:].bitcast(I32)), scalar1=HI_MASK, scalar2=None, op0=ALU.bitwise_and
         )
         nc.scalar.copy(out=w_bf[0][:, 0], in_=hi_bits[:].bitcast(F32))
-        nc.gpsimd.tensor_tensor(out=w_bf[0][:, 1], in0=woven(w_raw[0][:]), in1=hi_bits[:].bitcast(F32), op=ALU.subtract)
+        nc.gpsimd.tensor_tensor(out=w_bf[0][:, 1], in0=k_last(w_raw[0][:]), in1=hi_bits[:].bitcast(F32), op=ALU.subtract)
 
         v_scales = keep.tile([P, S], U8, name="v_scales", align_bytes=64)
         nc.vector.tensor_copy(out=v_scales[:], in_=lookup(scale_win[:].bitcast(U8), 0, S))
 
-        upper = keep.tile([P, P, PACK], BF16, name="upper", align_bytes=64)
+        upper = keep.tile([P, P, PACK], F32, name="upper")
         nc.scalar.copy(
-            out=upper[:], in_=w_raw[1][:].bitcast(BF16).rearrange("p j (n t) -> p n j t", t=2)[:, :, :, 1]
+            out=upper[:], in_=w_raw[1][:].bitcast(BF16).rearrange("p t (n e) -> p n t e", e=2)[:, :, :, 1]
         )
-        nc.vector.tensor_scalar(
-            out=w_bf[1][:, 0].rearrange("p n j -> p (n j)").bitcast(I32),
-            in0=upper[:].rearrange("p n j -> p (n j)").bitcast(I32),
-            scalar1=PAIR_MASK, scalar2=None, op0=ALU.bitwise_and,
-        )
-        nc.gpsimd.tensor_tensor(out=w_bf[1][:, 1], in0=woven(w_raw[1][:]), in1=w_bf[1][:, 0], op=ALU.subtract)
+        top = keep.tile([P, P, PACK], U32, name="top")
+        nc.scalar.activation(out=top[:], in_=upper[:].bitcast(U32), func=COPY, scale=2.0**-DROPPED_BITS, bias=ROUND_DOWN)
+        kept = keep.tile([P, P, PACK], U32, name="kept")
+        nc.scalar.activation(out=kept[:], in_=top[:], func=COPY, scale=2.0**DROPPED_BITS)
+        nc.gpsimd.tensor_tensor(out=w_bf[1][:, 1], in0=k_last(w_raw[1][:]), in1=kept[:].bitcast(F32), op=ALU.subtract)
+        nc.scalar.copy(out=w_bf[1][:, 0], in_=kept[:].bitcast(F32))
 
-        def quantize(m):
-            codes = keep.tile([P, 2 * P], U32, name=f"w_codes{m}", align_bytes=64)
-            scales = keep.tile([P, 2 * P], U8, name=f"w_scales{m}", align_bytes=64)
+        def quantize(half):
+            codes = keep.tile([P, 2 * P], U32, name=f"w_codes{half}", align_bytes=64)
+            scales = keep.tile([P, 2 * P], U8, name=f"w_scales{half}", align_bytes=64)
             nc.vector.quantize_mx(
-                out=codes[:].bitcast(FP8X4), scales=scales[:], in_=w_bf[m][:].rearrange("p h n j -> p (h n j)")
+                out=codes[:].bitcast(FP8X4), scales=scales[:], in_=w_bf[half][:].rearrange("p h n t -> p (h n t)")
             )
             return codes, scales
 
         first = quantize(0)
-        v_words = keep.tile([P, S], U32, name="v_words", tag="early", align_bytes=64)
-        for j0 in range(0, S, Q):
-            nc.vector.tensor_copy(out=v_words[:, j0 : j0 + Q], in_=lookup(word_win[:].bitcast(U32), j0, j0 + Q))
+        v_words = keep.tile([P, S], U32, name="v_words", tag="first_cut", align_bytes=64)
+        for j0 in range(0, S, WORD_PIECE):
+            j1 = j0 + WORD_PIECE
+            nc.vector.tensor_copy(out=v_words[:, j0:j1], in_=lookup(word_win[:].bitcast(U32), j0, j1))
         second = quantize(1)
 
-        def project(m, j0, j1, codes, scales, y_sb):
-            acc = psum.tile([P, j1 - j0], F32, name=f"acc{m}_{j0}")
+        def project(half, j0, j1, codes, scales, y_sb):
+            acc = psum.tile([P, j1 - j0], F32, name=f"acc{half}_{j0}")
             for part in range(2):
                 nc.tensor.matmul_mx(
                     out=acc[:],
@@ -104,16 +113,16 @@ def tile_list_tabres_none_kernel(tc, tab_words, tab_scales, w, rT, offs, out):
                 )
             nc.scalar.copy(out=y_sb[:, j0:j1], in_=acc[:])
 
-        def finish(m, j0, j1, y_sb, total):
-            nc.vector.tensor_tensor(out=total, in0=lookup(res_win[m][:], j0, j1), in1=y_sb[:, j0:j1], op=ALU.add)
-            nc.sync.dma_start(out=out[m * P : (m + 1) * P, j0:j1], in_=total)
+        def finish(half, j0, j1, y_sb, total):
+            nc.vector.tensor_tensor(
+                out=total[:, j0:j1], in0=lookup(res_win[half][:], j0, j1), in1=y_sb[:, j0:j1], op=ALU.add
+            )
+            nc.sync.dma_start(out=out[half * P : (half + 1) * P, j0:j1], in_=total[:, j0:j1])
 
-        for m, (codes, scales) in enumerate((first, second)):
-            y_sb = keep.tile([P, S], F32, name=f"y_sb{m}")
-            total = keep.tile([P, S], F32, name=f"total{m}")
-            cuts = PRODUCT_CUTS[m]
-            for j0, j1 in zip(cuts, cuts[1:]):
-                project(m, j0, j1, codes, scales, y_sb)
-            cuts = SUM_CUTS[m]
-            for j0, j1 in zip(cuts, cuts[1:]):
-                finish(m, j0, j1, y_sb, total[:, j0:j1])
+        for half, (codes, scales) in enumerate((first, second)):
+            y_sb = keep.tile([P, S], F32, name=f"y_sb{half}")
+            total = keep.tile([P, S], F32, name=f"total{half}")
+            for j0, j1 in zip(PRODUCT_CUTS[half], PRODUCT_CUTS[half][1:]):
+                project(half, j0, j1, codes, scales, y_sb)
+            for j0, j1 in zip(SUM_CUTS[half], SUM_CUTS[half][1:]):
+                finish(half, j0, j1, y_sb, total)

@@ -23,7 +23,7 @@ SCALE_ROWS = K // 32
 
 WORD_PIECE = 256
 PRODUCT_CUTS = ((0, 256, 512, 768, 1024), (0, 256, 512, 1024))
-SUM_CUTS = ((0, 256, 512, 1024), (0, 512, 896, 1024))
+SUM_CUTS = ((0, 256, 512, 1024), (0, 512, 832, 1024))
 
 DROPPED_BITS = 20
 HI_MASK = -(1 << DROPPED_BITS)

@@ -23,7 +23,7 @@ SCALE_ROWS = K // 32
 
 WORD_PIECE = 256
 PRODUCT_CUTS = ((0, 256, 512, 768, 1024), (0, 256, 512, 1024))
-SUM_CUTS = ((0, 256, 512, 1024), (0, 512, 832, 1024))
+SUM_CUTS = ((0, 256, 512, 768, 1024), (0, 512, 832, 1024))
 
 DROPPED_BITS = 20
 HI_MASK = -(1 << DROPPED_BITS)

@@ -24,6 +24,7 @@ SCALE_ROWS = K // 32
 WORD_PIECE = 256
 PRODUCT_CUTS = ((0, 256, 512, 768, 1024), (0, 256, 512, 1024))
 SUM_CUTS = ((0, 256, 512, 768, 1024), (0, 512, 832, 1024))
+STORE_CUTS = ((0, 256, 512, 1024), (0, 512, 832, 1024))
 
 DROPPED_BITS = 20
 HI_MASK = -(1 << DROPPED_BITS)
@@ -113,16 +114,19 @@ def tile_list_tabres_none_kernel(tc, tab_words, tab_scales, w, rT, offs, out):
                 )
             nc.scalar.copy(out=y_sb[:, j0:j1], in_=acc[:])
 
-        def finish(half, j0, j1, y_sb, total):
+        def add_residual(half, j0, j1, y_sb, total):
             nc.vector.tensor_tensor(
                 out=total[:, j0:j1], in0=lookup(res_win[half][:], j0, j1), in1=y_sb[:, j0:j1], op=ALU.add
             )
-            nc.sync.dma_start(out=out[half * P : (half + 1) * P, j0:j1], in_=total[:, j0:j1])
 
         for half, (codes, scales) in enumerate((first, second)):
             y_sb = keep.tile([P, S], F32, name=f"y_sb{half}")
             total = keep.tile([P, S], F32, name=f"total{half}")
             for j0, j1 in zip(PRODUCT_CUTS[half], PRODUCT_CUTS[half][1:]):
                 project(half, j0, j1, codes, scales, y_sb)
+            stored = 0
             for j0, j1 in zip(SUM_CUTS[half], SUM_CUTS[half][1:]):
-                finish(half, j0, j1, y_sb, total)
+                add_residual(half, j0, j1, y_sb, total)
+                if j1 in STORE_CUTS[half]:
+                    nc.sync.dma_start(out=out[half * P : (half + 1) * P, stored:j1], in_=total[:, stored:j1])
+                    stored = j1

@@ -26,6 +26,7 @@ PRODUCT_CUTS = ((0, 256, 512, 768, 1024), (0, 256, 512, 1024))
 SUM_CUTS = ((0, 256, 512, 768, 1024), (0, 512, 832, 1024))
 STORE_CUTS = ((0, 256, 512, 1024), (0, 512, 832, 1024))
 
+PIECE_BYTES = 4096
 DROPPED_BITS = 20
 HI_MASK = -(1 << DROPPED_BITS)
 ROUND_DOWN = -15.0 / 32.0
@@ -52,9 +53,9 @@ def tile_list_tabres_none_kernel(tc, tab_words, tab_scales, w, rT, offs, out):
         for r in range(4):
             nc.sync.dma_start(out=scale_win[r:P:QUADRANT, :], in_=scale_rows[r:SCALE_ROWS:4, :])
         nc.sync.dma_start(out=w_raw[1][:], in_=w_rows[:, :, P:M])
-        nc.sync.dma_start(out=word_win[:], in_=tab_words[0].rearrange("p c t -> p (c t)").bitcast(I32))
+        nc.sync.dma_start(out=word_win[:], in_=tab_words[0].rearrange("p c t -> p (c t)").bitcast(I32), max_dma_last_dim=PIECE_BYTES)
         for half in range(2):
-            nc.sync.dma_start(out=res_win[half][:], in_=rT[half * P : (half + 1) * P, :])
+            nc.sync.dma_start(out=res_win[half][:], in_=rT[half * P : (half + 1) * P, :], max_dma_last_dim=PIECE_BYTES)
 
         def lookup(window, j0, j1):
             return window.indirect(offsets[:, j0 // GROUP : j1 // GROUP])

from contextlib import ExitStack

import concourse.mybir as mybir

K, M, T, S = 512, 256, 2048, 1024
FLOPS = 2 * 2 * K * M * S

F32 = mybir.dt.float32
BF16 = mybir.dt.bfloat16
I32 = mybir.dt.int32
U32 = mybir.dt.uint32
U16 = mybir.dt.uint16
U8 = mybir.dt.uint8
FP8X4 = mybir.dt.float8_e4m3fn_x4
ALU = mybir.AluOpType
COPY = mybir.ActivationFunctionType.Copy

P = 128
PACK = 4
GROUP = 16
QUADRANT = 32
SCALE_ROWS = K // 32

WORD_PIECE = 256
PRODUCT_CUTS = ((0, 256, 512, 768, 1024), (0, 256, 512, 1024))
SUM_CUTS = ((0, 256, 512, 768, 1024), (0, 512, 832, 1024))
STORE_CUTS = ((0, 256, 512, 1024), (0, 512, 832, 1024))

PIECE_BYTES = 4096
DROPPED_BITS = 20
HI_MASK = -(1 << DROPPED_BITS)
ROUND_DOWN = -15.0 / 32.0


def tile_list_tabres_none_kernel(tc, tab_words, tab_scales, w, rT, offs, out):
    nc = tc.nc
    with ExitStack() as ctx:
        keep = ctx.enter_context(tc.tile_pool(name="keep", bufs=1))
        psum = ctx.enter_context(tc.psum_pool(name="psum", bufs=1))

        offsets = keep.tile([P, S // GROUP], U16, name="offsets")
        w_raw = [keep.tile([P, PACK, P], F32, name=f"w_raw{half}", tag=f"w_raw{half}") for half in range(2)]
        scale_win = keep.tile([P, T // 4], I32, name="scale_win")
        word_win = keep.tile([P, T], I32, name="word_win")
        res_win = [keep.tile([P, T], F32, name=f"res_win{half}") for half in range(2)]

        nc.vector.memset(scale_win[:], 0)

        w_rows = w.rearrange("(p t) n -> p t n", t=PACK)
        nc.sync.dma_start(out=w_raw[0][:], in_=w_rows[:, :, 0:P])
        nc.sync.dma_start(offsets[:], offs)
        scale_rows = tab_scales[0].bitcast(I32)
        for r in range(4):
            nc.sync.dma_start(out=scale_win[r:P:QUADRANT, :], in_=scale_rows[r:SCALE_ROWS:4, :])
        nc.sync.dma_start(out=w_raw[1][:], in_=w_rows[:, :, P:M])
        nc.sync.dma_start(out=word_win[:], in_=tab_words[0].rearrange("p c t -> p (c t)").bitcast(I32), max_dma_last_dim=PIECE_BYTES)
        for half in range(2):
            nc.sync.dma_start(out=res_win[half][:], in_=rT[half * P : (half + 1) * P, :], max_dma_last_dim=PIECE_BYTES)

        def lookup(window, j0, j1):
            return window.indirect(offsets[:, j0 // GROUP : j1 // GROUP])

        def k_last(view):
            return view.rearrange("p t n -> p n t")

        w_bf = [keep.tile([P, 2, P, PACK], BF16, name=f"w_bf{half}", align_bytes=64) for half in range(2)]

        hi_bits = keep.tile([P, P, PACK], I32, name="hi_bits", tag="first_cut", align_bytes=64)
        nc.vector.tensor_scalar(
            out=hi_bits[:], in0=k_last(w_raw[0][:].bitcast(I32)), scalar1=HI_MASK, scalar2=None, op0=ALU.bitwise_and
        )
        nc.scalar.copy(out=w_bf[0][:, 0], in_=hi_bits[:].bitcast(F32))
        nc.gpsimd.tensor_tensor(out=w_bf[0][:, 1], in0=k_last(w_raw[0][:]), in1=hi_bits[:].bitcast(F32), op=ALU.subtract)

        v_scales = keep.tile([P, S], U8, name="v_scales", align_bytes=64)
        nc.vector.tensor_copy(out=v_scales[:], in_=lookup(scale_win[:].bitcast(U8), 0, S))

        upper = keep.tile([P, P, PACK], F32, name="upper")
        nc.scalar.copy(
            out=upper[:], in_=w_raw[1][:].bitcast(BF16).rearrange("p t (n e) -> p n t e", e=2)[:, :, :, 1]
        )
        top = keep.tile([P, P, PACK], U32, name="top")
        nc.scalar.activation(out=top[:], in_=upper[:].bitcast(U32), func=COPY, scale=2.0**-DROPPED_BITS, bias=ROUND_DOWN)
        kept = keep.tile([P, P, PACK], U32, name="kept")
        nc.scalar.activation(out=kept[:], in_=top[:], func=COPY, scale=2.0**DROPPED_BITS)
        nc.gpsimd.tensor_tensor(out=w_bf[1][:, 1], in0=k_last(w_raw[1][:]), in1=kept[:].bitcast(F32), op=ALU.subtract)
        nc.scalar.copy(out=w_bf[1][:, 0], in_=kept[:].bitcast(F32))

        def quantize(half):
            codes = keep.tile([P, 2 * P], U32, name=f"w_codes{half}", align_bytes=64)
            scales = keep.tile([P, 2 * P], U8, name=f"w_scales{half}", align_bytes=64)
            nc.vector.quantize_mx(
                out=codes[:].bitcast(FP8X4), scales=scales[:], in_=w_bf[half][:].rearrange("p h n t -> p (h n t)")
            )
            return codes, scales

        first = quantize(0)
        v_words = keep.tile([P, S], U32, name="v_words", tag="first_cut", align_bytes=64)
        for j0 in range(0, S, WORD_PIECE):
            j1 = j0 + WORD_PIECE
            nc.vector.tensor_copy(out=v_words[:, j0:j1], in_=lookup(word_win[:].bitcast(U32), j0, j1))
        second = quantize(1)

        def project(half, j0, j1, codes, scales, y_sb):
            acc = psum.tile([P, j1 - j0], F32, name=f"acc{half}_{j0}")
            for part in range(2):
                nc.tensor.matmul_mx(
                    out=acc[:],
                    lhsT=codes[:, part * P : (part + 1) * P].bitcast(FP8X4),
                    lhsT_scale=scales[:, part * P : (part + 1) * P],
                    rhs=v_words[:, j0:j1].bitcast(FP8X4),
                    rhs_scale=v_scales[:, j0:j1],
                    start=(part == 0),
                    stop=(part == 1),
                )
            nc.scalar.copy(out=y_sb[:, j0:j1], in_=acc[:])

        def add_residual(half, j0, j1, y_sb, total):
            nc.vector.tensor_tensor(
                out=total[:, j0:j1], in0=lookup(res_win[half][:], j0, j1), in1=y_sb[:, j0:j1], op=ALU.add
            )

        for half, (codes, scales) in enumerate((first, second)):
            y_sb = keep.tile([P, S], F32, name=f"y_sb{half}")
            total = keep.tile([P, S], F32, name=f"total{half}")
            for j0, j1 in zip(PRODUCT_CUTS[half], PRODUCT_CUTS[half][1:]):
                project(half, j0, j1, codes, scales, y_sb)
            stored = 0
            for j0, j1 in zip(SUM_CUTS[half], SUM_CUTS[half][1:]):
                add_residual(half, j0, j1, y_sb, total)
                if j1 in STORE_CUTS[half]:
                    nc.sync.dma_start(out=out[half * P : (half + 1) * P, stored:j1], in_=total[:, stored:j1])
                    stored = j1
